import numpy as np
import ml_dtypes


def mxq(x, axis, fmt="e4m3"):
    dtype, down = {"e4m3": (ml_dtypes.float8_e4m3fn, 7), "e5m2": (ml_dtypes.float8_e5m2, 14)}[fmt]
    v = np.moveaxis(np.asarray(x, np.float32).astype(ml_dtypes.bfloat16).astype(np.float64), axis, -1)
    blocks = v.reshape(v.shape[:-1] + (-1, 32))
    amax = np.abs(blocks).max(-1, keepdims=True)
    byte = np.maximum(np.where(amax > 0, np.frexp(amax)[1] - 1 + 127, 0) - down, 1)
    scale = np.exp2(byte - 127.0)
    codes = (blocks / scale).astype(np.float32).astype(dtype).astype(np.float64)
    return np.moveaxis((codes * scale).reshape(v.shape), -1, axis)


WIDE = False


def mx_kscale(k):
    if not WIDE:
        return np.ones(k)
    levels = np.array([10, -10, 5, -5, 0])
    if k % 512:
        return np.exp2(np.random.permutation(np.resize(levels, k // 32))).repeat(32)
    a = np.empty((k // 512, 16))
    for p in range(k // 512):
        a[p, :8] = np.random.permutation(np.resize(levels, 8))
        for g in range(8):
            far = levels[np.abs(levels - a[p, g]) >= 10]
            a[p, g + 8] = far[np.random.randint(len(far))]
    return np.exp2(a.ravel()).repeat(32)


def f64(x):
    return np.asarray(x).astype(np.float64)


def striped(idx):
    return np.tile(idx.reshape(-1, 16).T, (8, 1)).astype(np.uint16)


def unstriped(offs):
    return offs[:16].T.reshape(-1).astype(np.int64)


E2M1 = np.array([0.0, 0.5, 1.0, 1.5, 2.0, 3.0, 4.0, 6.0, -0.0, -0.5, -1.0, -1.5, -2.0, -3.0, -4.0, -6.0])


def pack_weight(w, fmt):
    k, n = w.shape
    w = f64(np.asarray(w, np.float32).astype(ml_dtypes.bfloat16)).reshape(k // 32, 32, n)
    amax = np.abs(w).max(1)
    if fmt == "e4m3":
        byte = np.frexp(amax)[1] - 1 + 127 - 7
    else:
        mant, ex = np.frexp(amax / 6.0)
        byte = np.where(mant > 0.5, ex, ex - 1) + 127
    byte = np.clip(np.where(amax > 0, byte, 1), 1, 254)
    scaled = (w * np.exp2(127.0 - byte)[:, None, :]).reshape(k, n).astype(np.float32)
    by_word = np.ascontiguousarray(scaled.reshape(k // 512, 128, 4, n).transpose(0, 1, 3, 2))
    if fmt == "e4m3":
        words = by_word.astype(ml_dtypes.float8_e4m3fn).view(np.uint8)
    else:
        c = by_word.astype(ml_dtypes.float4_e2m1fn).view(np.uint8) & 0xF
        words = (c[..., 0::2] | (c[..., 1::2] << 4)).reshape(k // 512, 128, 2 * n)
    return np.ascontiguousarray(words), np.ascontiguousarray(byte.astype(np.uint8).reshape(k // 512, 16, n))


def unpack_weight(words, scales, fmt):
    g, _, n = scales.shape
    words = np.ascontiguousarray(words).reshape(g, 128, n, -1)
    if fmt == "e4m3":
        vals = words.view(ml_dtypes.float8_e4m3fn).astype(np.float64)
    else:
        nib = np.empty((g, 128, n, 4), np.uint8)
        nib[..., 0::2] = words & 0xF
        nib[..., 1::2] = words >> 4
        vals = E2M1[nib]
    vals = vals * np.repeat(np.exp2(scales.astype(np.float64) - 127.0), 8, axis=1)[..., None]
    return vals.transpose(0, 1, 3, 2).reshape(g * 512, n)


def gelu(v):
    return 0.5 * v * (1.0 + np.tanh(np.sqrt(2.0 / np.pi) * (v + 0.044715 * v**3)))


K, H, T, S, T3, S2, T2 = 1024, 1024, 2048, 512, 1024, 512, 1024

def setup_inputs():
    n = np.random.standard_normal
    u = mx_kscale(K)[:, None]
    tab_words, tab_scales = pack_weight(n((K, T)) * u, "e4m3")
    tab2_words, tab2_scales = pack_weight(n((H, T3)) / np.sqrt(H) / u, "e4m3")
    w1_words, w1_scales = pack_weight(1.2 * n((K, H)) / np.sqrt(K) / u, "e2m1")
    return {
        "tab_words": tab_words, "tab_scales": tab_scales,
        "offs": striped(np.random.permutation(T)[:S]),
        "tab2_words": tab2_words, "tab2_scales": tab2_scales,
        "offs2": striped(np.random.permutation(T3)[:S2]),
        "offs3": striped(np.random.permutation(T2)[:S]),
        "w1_words": w1_words, "w1_scales": w1_scales,
        "b1": (0.6 * n(H)).astype(np.float32),
        "w2": (0.55 * n((K, H)) / np.sqrt(K) / u).astype(np.float32),
        "gain": (2.0 * np.exp(0.3 * n(H)) * u[:, 0]).astype(np.float32),
        "em": (0.55 * np.exp(0.3 * n(S2))).astype(np.float32),
        "page1": (0.5 * n((S2, T2))).astype(np.float32),
        "wgo": np.exp(0.3 * n((128, S))).astype(np.float32),
    }

def reference(tab_words, tab_scales, offs, tab2_words, tab2_scales, offs2, offs3, w1_words, w1_scales, b1, w2, gain, em, page1, wgo):
    v = unpack_weight(tab_words, tab_scales, "e4m3")[:, unstriped(offs)]
    v2 = unpack_weight(tab2_words, tab2_scales, "e4m3")[:, unstriped(offs2)]
    w1 = unpack_weight(w1_words, w1_scales, "e2m1")
    w2q = mxq(f64(w2), 0, "e4m3")
    bent = np.tanh((w1.T @ v) + f64(b1)[:, None])
    wave = np.sin(w2q.T @ v)
    h = f64(gain)[:, None] * (bent + wave)
    hq = mxq(h, 0, "e4m3")
    e = v2.T @ hq + v2.T @ v
    score = np.tanh(f64(em)[:, None] * e)
    out = f64(page1).copy()
    out[:, unstriped(offs3)] = np.tile(f64(wgo), (S2 // 128, 1)) * score
    return out

@@ -1,0 +1,318 @@
+import math
+from contextlib import ExitStack
+
+import concourse.mybir as mybir
+
+F32 = mybir.dt.float32
+BF16 = mybir.dt.bfloat16
+I32 = mybir.dt.int32
+U32 = mybir.dt.uint32
+U16 = mybir.dt.uint16
+U8 = mybir.dt.uint8
+FP8X4 = mybir.dt.float8_e4m3fn_x4
+FP4X4 = mybir.dt.float4_e2m1fn_x4
+ACT = mybir.ActivationFunctionType
+ALU = mybir.AluOpType
+
+P = 128
+PACK = 4
+K_PASS = 512
+PASSES = 2
+K, H, T, S, T3, S2, T2 = 1024, 1024, 2048, 512, 1024, 512, 1024
+BANK = 512
+QUADS = 4
+SLICES = ((0, 256), (256, 256))
+WARM = True
+LOADS = "idx:s tab0:s ts:s w1:s w1sa:s w1sb:s tab1:s b1:s gain:s c0:s c1:s idx2:s t2s:s em:s c2:s c3:s tab2:s idx3:s wgo:s pages:s"
+BG_SCALAR = (0, 0, 0, 0)
+FIRST = 512
+WAVE_TAG = ("wide2", "wide3")
+WAVE_AGAIN = False
+HB_TAG = ("half3", "half2", "half0", "score10")
+PACKED = False
+SHIFT_Q = "a"
+BG_TAG = (0, 1)
+STAGE = 3
+WAVES = 3
+ORDER = "Q0 Q1 Q2 Q3 W0 W1 F00 F10 G04 S00 S10 F01 F11 S20 S30 S01 S11 S21 S31"
+NB = (3, 3, 2)
+CAST_SCALAR = (0, 0, 128, 32)
+
+FLOPS = 2 * K * H * S * 2 + 2 * H * S2 * S * 2
+
+
+def tile_list_ballroom_exemplar_scores_kernel(
+    tc, tab_words, tab_scales, offs, tab2_words, tab2_scales, offs2, offs3, w1_words, w1_scales, b1, w2, gain, em, page1, wgo, out
+):
+    nc = tc.nc
+    with ExitStack() as ctx:
+        keep = ctx.enter_context(tc.tile_pool(name="keep", bufs=1))
+        ring = ctx.enter_context(tc.tile_pool(name="ring", bufs=2))
+        psum = ctx.enter_context(tc.psum_pool(name="psum", bufs=1))
+
+        def held(name, shape, dtype):
+            return keep.tile(shape, dtype, name=name, align_bytes=64)
+
+        idx = held("idx", [P, S // 16], U16)
+        idx2 = held("idx2", [P, S2 // 16], U16)
+        idx3 = held("idx3", [P, S // 16], U16)
+        w1_raw = held("w1_raw", [P, PASSES, H], U16)
+        w1_codes = held("w1_codes", [P, PASSES, H], U16)
+        w1_raw_scales = held("w1_raw_scales", [P, PASSES, H], U8)
+        w1_planes = held("w1_planes", [P, PASSES, H], U8)
+        tab = [held(f"tab{a}", [P, T], I32) for a in range(PASSES)]
+        tab_planes = held("tab_planes", [P, T] if PACKED else [P, PASSES, T], U8)
+        tab2 = held("tab2", [P, PASSES, T3], I32)
+        tab2_planes = held("tab2_planes", [P, T3], U8)
+        v_codes = [held(f"v_codes{a}", [P, S], I32) for a in range(PASSES)]
+        v_planes = [held(f"v_planes{a}", [P, S], U8) for a in range(PASSES)]
+        v2_codes = [held(f"v2_codes{a}", [P, S2], I32) for a in range(PASSES)]
+        v2_planes = held("v2_planes", [P, S2], U8)
+        chunks = [(b, a) for b in range(PASSES) for a in range(PASSES)]
+        w2_raw = {c: keep.tile([P, PACK, K_PASS], F32, name=f"w2_raw{c[0]}{c[1]}", tag=f"wide{i}", align_bytes=64) for i, c in enumerate(chunks)}
+        w2_bf = {c: keep.tile([P, K_PASS * PACK], BF16, name=f"w2_bf{c[0]}{c[1]}", tag=f"half{i}", align_bytes=64) for i, c in enumerate(chunks)}
+        w2_codes = {c: held(f"w2_codes{c[0]}{c[1]}", [P, K_PASS], U32) for c in chunks}
+        w2_planes = {c: held(f"w2_planes{c[0]}{c[1]}", [P, K_PASS], U8) for c in chunks}
+        pages = [held(f"page{m}", [P, T2], F32) for m in range(S2 // P)]
+        wgo_sb = held("wgo_sb", [P, S], F32)
+        gain_sb = held("gain_sb", [P, PASSES, PACK], F32)
+        b1_sb = held("b1_sb", [P, PASSES, PACK], F32)
+        em_sb = held("em_sb", [P, S2 // P], F32)
+        ones = held("ones", [P, 8], F32)
+        halves = held("halves", [P, 8], F32)
+        quarter_pi = held("quarter_pi", [P, 8], F32)
+        half_sign = held("half_sign", [P, 8], F32)
+        half_abs = held("half_abs", [P, 8], F32)
+        twice_abs = held("twice_abs", [P, 8], F32)
+        minus_abs = held("minus_abs", [P, 8], F32)
+        root = held("root", [P, 8], F32)
+        bent = [held(f"bent{b}", [P, PACK, S], F32) for b in range(PASSES)]
+
+        nc.vector.memset((tab_planes[:] if PACKED else tab_planes[:].rearrange("p a t -> p (a t)")).bitcast(I32), 0)
+        nc.vector.memset(w1_raw_scales[:].rearrange("p a t -> p (a t)").bitcast(I32), 0)
+        nc.gpsimd.memset(tab2_planes[:].bitcast(I32), 0)
+        nc.vector.memset(ones[:], 1.0)
+        nc.vector.memset(halves[:], 0.5)
+        if WARM:
+            warm = held("warm", [P, 1], F32)
+            nc.scalar.activation(out=warm[:], in_=ones[:, 0:1], func=ACT.Silu)
+
+        def load_w2(c):
+            b, a = c
+            nc.sync.dma_start(
+                out=w2_raw[c][:],
+                in_=w2[a * K_PASS : (a + 1) * K_PASS, b * K_PASS : (b + 1) * K_PASS].rearrange("(p k) r -> p k r", k=PACK),
+            )
+
+        queues = {"s": nc.sync, "a": nc.scalar, "g": nc.gpsimd}
+
+        def load(name, q):
+            eng = queues[q]
+            if name == "idx":
+                nc.sync.dma_start(idx[:], offs)
+            elif name == "idx2":
+                nc.sync.dma_start(idx2[:], offs2)
+            elif name == "idx3":
+                nc.sync.dma_start(idx3[:], offs3)
+            elif name == "w1":
+                eng.dma_start(out=w1_raw[:].bitcast(I32), in_=w1_words.rearrange("a p c -> p a c").bitcast(I32))
+            elif name in ("tab0", "tab1"):
+                a = int(name[3:])
+                eng.dma_start(out=tab[a][:], in_=tab_words[a].rearrange("p t i -> p (t i)").bitcast(I32))
+            elif name == "ts" and PACKED:
+                for k in range(QUADS):
+                    eng.dma_start(out=tab_planes[32 * k : 32 * k + 8, :].bitcast(I32), in_=tab_scales[:, 4 * k : 4 * k + 4, :].bitcast(I32))
+            elif name == "ts":
+                for k in range(QUADS):
+                    eng.dma_start(
+                        out=tab_planes[32 * k : 32 * k + 4, :, :].bitcast(I32),
+                        in_=tab_scales[:, 4 * k : 4 * k + 4, :].rearrange("a r t -> r a t").bitcast(I32),
+                    )
+            elif name in ("w1sa", "w1sb"):
+                for k in ((0, 1) if name == "w1sa" else (2, 3)):
+                    eng.dma_start(
+                        out=w1_raw_scales[32 * k : 32 * k + 4, :, :].bitcast(I32),
+                        in_=w1_scales[:, 4 * k : 4 * k + 4, :].rearrange("a r t -> r a t").bitcast(I32),
+                    )
+            elif name == "t2s":
+                for k in range(QUADS):
+                    eng.dma_start(
+                        out=tab2_planes[32 * k : 32 * k + 8, :].bitcast(I32),
+                        in_=tab2_scales[:, 4 * k : 4 * k + 4, :].bitcast(I32),
+                    )
+            elif name == "gain":
+                eng.dma_start(out=gain_sb[:], in_=gain.rearrange("(b p t) -> p b t", p=P, t=PACK))
+            elif name == "b1":
+                eng.dma_start(out=b1_sb[:], in_=b1.rearrange("(b p t) -> p b t", p=P, t=PACK))
+            elif name == "em":
+                with nc.allow_non_contiguous_dma(reason="one factor for each partition"):
+                    eng.dma_start(out=em_sb[:], in_=em.rearrange("(m p) -> p m", p=P))
+            elif name in ("c0", "c1", "c2", "c3"):
+                load_w2(chunks[int(name[1:])])
+            elif name == "tab2":
+                eng.dma_start(out=tab2[:], in_=tab2_words.rearrange("a p t i -> p a (t i)").bitcast(I32))
+            elif name == "wgo":
+                eng.dma_start(out=wgo_sb[:], in_=wgo)
+            else:
+                for m in range(S2 // P):
+                    eng.dma_start(out=pages[m][:], in_=page1[m * P : (m + 1) * P, :])
+
+        for item in LOADS.split():
+            load(*item.split(":"))
+
+        gain_flat = gain_sb[:].rearrange("p b t -> p (b t)")
+        nc.gpsimd.tensor_scalar(quarter_pi[:], ones[:], math.pi / 4, 0.0, ALU.mult, ALU.add)
+        nc.gpsimd.tensor_scalar(half_sign[:], gain_flat, 0.0, -0.5, ALU.is_ge, ALU.add)
+        nc.gpsimd.tensor_tensor(half_abs[:], gain_flat, half_sign[:], ALU.mult)
+        nc.gpsimd.tensor_scalar(twice_abs[:], half_abs[:], 4.0, 0.0, ALU.mult, ALU.add)
+        nc.gpsimd.tensor_scalar(minus_abs[:], half_abs[:], -2.0, 0.0, ALU.mult, ALU.add)
+        nc.gpsimd.tensor_tensor(root[:], twice_abs[:], halves[:], ALU.pow)
+
+        nc.scalar.copy(
+            out=w1_codes[:].rearrange("p a (b t m) -> p (a b) t m", t=PACK, m=P),
+            in_=w1_raw[:].rearrange("p a (b m t) -> p (a b) t m", t=PACK, m=P),
+        )
+        def gather_v(j0, j1):
+            part = idx[:, j0 // 16 : j1 // 16]
+            nc.vector.tensor_copy(v_codes[0][:, j0:j1].bitcast(U32), tab[0][:].bitcast(U32).indirect(part))
+            if PACKED:
+                nc.vector.tensor_copy(v_planes[0][:, j0:j1], tab_planes[:].indirect(part))
+                queues[SHIFT_Q].dma_start(out=v_planes[1][0 : P - 4, j0:j1].bitcast(I32), in_=v_planes[0][4:P, j0:j1].bitcast(I32))
+            else:
+                for a in range(PASSES):
+                    nc.vector.tensor_copy(v_planes[a][:, j0:j1], tab_planes[:, a, :].indirect(part))
+            if j0 == 0:
+                nc.vector.tensor_copy(
+                    out=w1_planes[:].rearrange("p a (b t m) -> p (a b) t m", t=PACK, m=P),
+                    in_=w1_raw_scales[:].rearrange("p a (b m t) -> p (a b) t m", t=PACK, m=P),
+                )
+            nc.vector.tensor_copy(v_codes[1][:, j0:j1].bitcast(U32), tab[1][:].bitcast(U32).indirect(part))
+
+        gather_v(0, FIRST)
+        if FIRST < S:
+            gather_v(FIRST, S)
+        nc.vector.tensor_copy(v2_planes[:], tab2_planes[:].indirect(idx2[:]))
+
+        def quantize_w2(c):
+            n_s = CAST_SCALAR[chunks.index(c)]
+            src = w2_raw[c][:].rearrange("p k (m t) -> p m k t", t=PACK)
+            dst = w2_bf[c][:].rearrange("p (t m k) -> p m k t", t=PACK, k=PACK)
+            if n_s > 0:
+                nc.scalar.copy(out=dst[:, 0:n_s], in_=src[:, 0:n_s])
+            if n_s < P:
+                nc.vector.tensor_copy(out=dst[:, n_s:P], in_=src[:, n_s:P])
+            nc.vector.quantize_mx(out=w2_codes[c][:].bitcast(FP8X4), scales=w2_planes[c][:], in_=w2_bf[c][:])
+
+        scaled = {}
+
+        def bend(b, j0, n):
+            per_bank = BANK // n
+            for t0 in range(0, PACK, per_bank):
+                acc = psum.tile([P, per_bank, n], F32, name="acc1", tag="acc1", bufs=NB[0])
+                for u in range(per_bank):
+                    cols = slice(b * K_PASS + (t0 + u) * P, b * K_PASS + (t0 + u + 1) * P)
+                    for a in range(PASSES):
+                        nc.tensor.matmul_mx(
+                            out=acc[:, u, :],
+                            lhsT=w1_codes[:, a, cols].bitcast(FP4X4),
+                            lhsT_scale=w1_planes[:, a, cols],
+                            rhs=v_codes[a][:, j0 : j0 + n].bitcast(FP8X4),
+                            rhs_scale=v_planes[a][:, j0 : j0 + n],
+                            start=(a == 0),
+                            stop=(a == PASSES - 1),
+                        )
+                for u in range(per_bank):
+                    t = t0 + u
+                    nc.scalar.activation(out=bent[b][:, t, j0 : j0 + n], in_=acc[:, u, :], func=ACT.Tanh, bias=b1_sb[:, b, t : t + 1])
+            for t in range(PACK):
+                ch = b * PACK + t
+                if b not in scaled:
+                    scaled[b] = keep.tile([P, PACK, S], F32, name=f"scaled{b}", tag=f"wide{BG_TAG[b]}", align_bytes=64)
+                part = bent[b][:, t, j0 : j0 + n]
+                dest = scaled[b][:, t, j0 : j0 + n]
+                if BG_SCALAR[[j for j, w in SLICES].index(j0)]:
+                    nc.scalar.activation(out=dest, in_=part, func=ACT.Identity, scale=gain_sb[:, b, t : t + 1], bias=minus_abs[:, ch : ch + 1])
+                else:
+                    nc.vector.tensor_scalar(dest, part, gain_sb[:, b, t : t + 1], minus_abs[:, ch : ch + 1], ALU.mult, ALU.add)
+
+        h_codes = {}
+        h_planes = {}
+
+        def features(b, j0, n):
+            per_bank = BANK // n
+            wave = keep.tile([P, PACK, n], F32, name="wave", tag=WAVE_TAG[b] if j0 == 0 or WAVE_AGAIN else f"wave{b}", align_bytes=64)
+            for t0 in range(0, PACK, per_bank):
+                acc = psum.tile([P, per_bank, n], F32, name="acc2", tag="acc2", bufs=NB[1])
+                for u in range(per_bank):
+                    cols = slice((t0 + u) * P, (t0 + u + 1) * P)
+                    for a in range(PASSES):
+                        nc.tensor.matmul_mx(
+                            out=acc[:, u, :],
+                            lhsT=w2_codes[(b, a)][:, cols].bitcast(FP8X4),
+                            lhsT_scale=w2_planes[(b, a)][:, cols],
+                            rhs=v_codes[a][:, j0 : j0 + n].bitcast(FP8X4),
+                            rhs_scale=v_planes[a][:, j0 : j0 + n],
+                            start=(a == 0),
+                            stop=(a == PASSES - 1),
+                        )
+                for u in range(per_bank):
+                    t = t0 + u
+                    ch = b * PACK + t
+                    nc.scalar.activation(
+                        out=wave[:, t, :], in_=acc[:, u, :], func=ACT.Sin, scale=half_sign[:, ch : ch + 1], bias=quarter_pi[:, 0:1]
+                    )
+                for u in range(per_bank):
+                    t = t0 + u
+                    ch = b * PACK + t
+                    nc.scalar.activation(out=wave[:, t, :], in_=wave[:, t, :], func=ACT.Square, scale=root[:, ch : ch + 1])
+            h_bf = keep.tile([P, n * PACK], BF16, name="h_bf", tag=HB_TAG[2 * [j for j, w in SLICES].index(j0) + b], align_bytes=64)
+            nc.vector.tensor_tensor(
+                h_bf[:].rearrange("p (c i t) -> p c t i", i=2, t=PACK),
+                wave[:].rearrange("p t (c i) -> p c t i", i=2),
+                scaled[b][:, :, j0 : j0 + n].rearrange("p t (c i) -> p c t i", i=2),
+                ALU.add,
+            )
+            h_codes[(b, j0)] = held(f"h_codes{b}_{j0}", [P, n], U32)
+            h_planes[(b, j0)] = held(f"h_planes{b}_{j0}", [P, n], U8)
+            nc.vector.quantize_mx(out=h_codes[(b, j0)][:].bitcast(FP8X4), scales=h_planes[(b, j0)][:], in_=h_bf[:])
+
+        def scores(m, j0, n):
+            rows = slice(m * P, (m + 1) * P)
+            acc = psum.tile([P, n], F32, name="acc3", tag="acc3", bufs=NB[2])
+            moving = [(a, v_codes[a][:, j0 : j0 + n], v_planes[a][:, j0 : j0 + n]) for a in range(PASSES)]
+            moving = moving + [(a, h_codes[(a, j0)][:], h_planes[(a, j0)][:]) for a in range(PASSES)]
+            for i, (a, codes, planes) in enumerate(moving):
+                nc.tensor.matmul_mx(
+                    out=acc[:],
+                    lhsT=v2_codes[a][:, rows].bitcast(FP8X4),
+                    lhsT_scale=v2_planes[4 * a : P, rows],
+                    rhs=codes.bitcast(FP8X4),
+                    rhs_scale=planes,
+                    start=(i == 0),
+                    stop=(i == len(moving) - 1),
+                )
+            score = keep.tile([P, n], F32, name="score", tag=f"score{m}{[j for j, w in SLICES].index(j0)}", align_bytes=64)
+            nc.scalar.activation(out=score[:], in_=acc[:], func=ACT.Tanh, scale=em_sb[:, m : m + 1])
+            nc.vector.tensor_tensor(pages[m][:].indirect(idx3[:, j0 // 16 : (j0 + n) // 16]), score[:], wgo_sb[:, j0 : j0 + n], ALU.mult)
+
+        for tok in ORDER.split():
+            kind = tok[0]
+            if kind == "W":
+                bend(int(tok[1]), 0, S)
+            elif kind == "A":
+                bend(int(tok[1]), *SLICES[int(tok[2])])
+            elif kind == "Q":
+                quantize_w2(chunks[int(tok[1])])
+            elif kind == "F":
+                features(int(tok[1]), *SLICES[int(tok[2])])
+            elif kind == "G":
+                for a in range(PASSES):
+                    m0, m1 = int(tok[1]), int(tok[2])
+                    nc.vector.tensor_copy(
+                        v2_codes[a][:, m0 * P : m1 * P].bitcast(U32), tab2[:, a, :].bitcast(U32).indirect(idx2[:, m0 * 8 : m1 * 8])
+                    )
+            else:
+                m = int(tok[1])
+                scores(m, *SLICES[int(tok[2])])
+                if int(tok[2]) == len(SLICES) - 1:
+                    nc.sync.dma_start(out=out[m * P : (m + 1) * P, :], in_=pages[m][:])

@@ -23,7 +23,7 @@ BANK = 512
 QUADS = 4
 SLICES = ((0, 256), (256, 256))
 WARM = True
-LOADS = "idx:s tab0:s ts:s w1:s w1sa:s w1sb:s tab1:s b1:s gain:s c0:s c1:s idx2:s t2s:s em:s c2:s c3:s tab2:s idx3:s wgo:s pages:s"
+LOADS = "gain:s idx:s b1:g em:g tab0:s ts:s w1:s w1sa:s w1sb:s tab1:s idx2:s t2s:s c0:s c1:s c2:s c3:s tab2:s idx3:s wgo:s pages:s"
 BG_SCALAR = (0, 0, 0, 0)
 FIRST = 512
 WAVE_TAG = ("wide2", "wide3")
@@ -79,7 +79,10 @@ def tile_list_ballroom_exemplar_scores_kernel(
         b1_sb = held("b1_sb", [P, PASSES, PACK], F32)
         em_sb = held("em_sb", [P, S2 // P], F32)
         ones = held("ones", [P, 8], F32)
-        halves = held("halves", [P, 8], F32)
+        tiny = held("tiny", [P, 8], F32)
+        guess = held("guess", [P, 8], F32)
+        rough = held("rough", [P, 8], F32)
+        step = held("step", [P, 8], F32)
         quarter_pi = held("quarter_pi", [P, 8], F32)
         half_sign = held("half_sign", [P, 8], F32)
         half_abs = held("half_abs", [P, 8], F32)
@@ -90,12 +93,10 @@ def tile_list_ballroom_exemplar_scores_kernel(
 
         nc.vector.memset((tab_planes[:] if PACKED else tab_planes[:].rearrange("p a t -> p (a t)")).bitcast(I32), 0)
         nc.vector.memset(w1_raw_scales[:].rearrange("p a t -> p (a t)").bitcast(I32), 0)
-        nc.gpsimd.memset(tab2_planes[:].bitcast(I32), 0)
+        nc.vector.memset(tab2_planes[:].bitcast(I32), 0)
         nc.vector.memset(ones[:], 1.0)
-        nc.vector.memset(halves[:], 0.5)
-        if WARM:
-            warm = held("warm", [P, 1], F32)
-            nc.scalar.activation(out=warm[:], in_=ones[:, 0:1], func=ACT.Silu)
+        nc.vector.tensor_scalar(tiny[:], ones[:], 1e-30, None, ALU.mult)
+        nc.vector.tensor_scalar(quarter_pi[:], ones[:], math.pi / 4, None, ALU.mult)
 
         def load_w2(c):
             b, a = c
@@ -161,12 +162,18 @@ def tile_list_ballroom_exemplar_scores_kernel(
             load(*item.split(":"))
 
         gain_flat = gain_sb[:].rearrange("p b t -> p (b t)")
-        nc.gpsimd.tensor_scalar(quarter_pi[:], ones[:], math.pi / 4, 0.0, ALU.mult, ALU.add)
         nc.gpsimd.tensor_scalar(half_sign[:], gain_flat, 0.0, -0.5, ALU.is_ge, ALU.add)
         nc.gpsimd.tensor_tensor(half_abs[:], gain_flat, half_sign[:], ALU.mult)
         nc.gpsimd.tensor_scalar(twice_abs[:], half_abs[:], 4.0, 0.0, ALU.mult, ALU.add)
         nc.gpsimd.tensor_scalar(minus_abs[:], half_abs[:], -2.0, 0.0, ALU.mult, ALU.add)
-        nc.gpsimd.tensor_tensor(root[:], twice_abs[:], halves[:], ALU.pow)
+        nc.scalar.activation(out=guess[:], in_=gain_flat, func=ACT.Abs_reciprocal_sqrt, scale=2.0, bias=tiny[:, 0:1])
+        if WARM:
+            warm = held("warm", [P, 1], F32)
+            nc.scalar.activation(out=warm[:], in_=guess[:, 0:1], func=ACT.Silu)
+        nc.gpsimd.tensor_tensor(rough[:], twice_abs[:], guess[:], ALU.mult)
+        nc.gpsimd.tensor_tensor(step[:], rough[:], guess[:], ALU.mult)
+        nc.gpsimd.tensor_scalar(step[:], step[:], -0.5, 1.5, ALU.mult, ALU.add)
+        nc.gpsimd.tensor_tensor(root[:], rough[:], step[:], ALU.mult)
 
         nc.scalar.copy(
             out=w1_codes[:].rearrange("p a (b t m) -> p (a b) t m", t=PACK, m=P),
@@ -195,12 +202,12 @@ def tile_list_ballroom_exemplar_scores_kernel(
 
         def quantize_w2(c):
             n_s = CAST_SCALAR[chunks.index(c)]
-            src = w2_raw[c][:].rearrange("p k (m t) -> p m k t", t=PACK)
-            dst = w2_bf[c][:].rearrange("p (t m k) -> p m k t", t=PACK, k=PACK)
+            src = w2_raw[c][:].rearrange("p k (m u t) -> p u m k t", u=2, t=2)
+            dst = w2_bf[c][:].rearrange("p (u t m k) -> p u m k t", u=2, t=2, k=PACK)
             if n_s > 0:
-                nc.scalar.copy(out=dst[:, 0:n_s], in_=src[:, 0:n_s])
+                nc.scalar.copy(out=dst[:, :, 0:n_s], in_=src[:, :, 0:n_s])
             if n_s < P:
-                nc.vector.tensor_copy(out=dst[:, n_s:P], in_=src[:, n_s:P])
+                nc.vector.tensor_copy(out=dst[:, :, n_s:P], in_=src[:, :, n_s:P])
             nc.vector.quantize_mx(out=w2_codes[c][:].bitcast(FP8X4), scales=w2_planes[c][:], in_=w2_bf[c][:])
 
         scaled = {}

@@ -24,17 +24,17 @@ QUADS = 4
 SLICES = ((0, 256), (256, 256))
 WARM = True
 LOADS = "gain:s idx:s b1:g em:g tab0:s ts:s w1:s w1sa:s w1sb:s tab1:s idx2:s t2s:s c0:s c1:s c2:s c3:s tab2:s idx3:s wgo:s pages:s"
-BG_SCALAR = (0, 0, 0, 0)
 FIRST = 512
 WAVE_TAG = ("wide2", "wide3")
 WAVE_AGAIN = False
 HB_TAG = ("half3", "half2", "half0", "score10")
 PACKED = False
 SHIFT_Q = "a"
-BG_TAG = (0, 1)
+BG_TAG = ("wide0", "wide1", "half0", "half1")
+SC_TAG = {(3, 0): "wave1", (1, 0): "wave0"}
 STAGE = 3
 WAVES = 3
-ORDER = "Q0 Q1 Q2 Q3 W0 W1 F00 F10 G04 S00 S10 F01 F11 S20 S30 S01 S11 S21 S31"
+ORDER = "Q0 Q1 Q2 Q3 W0 W1 Bv09 Bv19 F00 F10 G04 F01 S00 S10 F11 S20 S30 S01 S11 S21 S31"
 NB = (3, 3, 2)
 CAST_SCALAR = (0, 0, 128, 32)
 
@@ -231,13 +231,18 @@ def tile_list_ballroom_exemplar_scores_kernel(
                 for u in range(per_bank):
                     t = t0 + u
                     nc.scalar.activation(out=bent[b][:, t, j0 : j0 + n], in_=acc[:, u, :], func=ACT.Tanh, bias=b1_sb[:, b, t : t + 1])
+
+        def scale_bent(b, i, on_scalar):
+            j0, n = SLICES[i] if i < 9 else (0, S)
+            whole = keep.tile([P, PACK, n], F32, name=f"scaled{b}{i}", tag=BG_TAG[2 * (i % 9) + b], align_bytes=64)
+            for j, w in SLICES:
+                if j0 <= j < j0 + n:
+                    scaled[(b, j)] = whole[:, :, j - j0 : j - j0 + w]
             for t in range(PACK):
                 ch = b * PACK + t
-                if b not in scaled:
-                    scaled[b] = keep.tile([P, PACK, S], F32, name=f"scaled{b}", tag=f"wide{BG_TAG[b]}", align_bytes=64)
                 part = bent[b][:, t, j0 : j0 + n]
-                dest = scaled[b][:, t, j0 : j0 + n]
-                if BG_SCALAR[[j for j, w in SLICES].index(j0)]:
+                dest = whole[:, t, :]
+                if on_scalar:
                     nc.scalar.activation(out=dest, in_=part, func=ACT.Identity, scale=gain_sb[:, b, t : t + 1], bias=minus_abs[:, ch : ch + 1])
                 else:
                     nc.vector.tensor_scalar(dest, part, gain_sb[:, b, t : t + 1], minus_abs[:, ch : ch + 1], ALU.mult, ALU.add)
@@ -276,7 +281,7 @@ def tile_list_ballroom_exemplar_scores_kernel(
             nc.vector.tensor_tensor(
                 h_bf[:].rearrange("p (c i t) -> p c t i", i=2, t=PACK),
                 wave[:].rearrange("p t (c i) -> p c t i", i=2),
-                scaled[b][:, :, j0 : j0 + n].rearrange("p t (c i) -> p c t i", i=2),
+                scaled[(b, j0)].rearrange("p t (c i) -> p c t i", i=2),
                 ALU.add,
             )
             h_codes[(b, j0)] = held(f"h_codes{b}_{j0}", [P, n], U32)
@@ -298,13 +303,15 @@ def tile_list_ballroom_exemplar_scores_kernel(
                     start=(i == 0),
                     stop=(i == len(moving) - 1),
                 )
-            score = keep.tile([P, n], F32, name="score", tag=f"score{m}{[j for j, w in SLICES].index(j0)}", align_bytes=64)
+            score = keep.tile([P, n], F32, name="score", tag=SC_TAG.get((m, j0), f"score{m}{[j for j, w in SLICES].index(j0)}"), align_bytes=64)
             nc.scalar.activation(out=score[:], in_=acc[:], func=ACT.Tanh, scale=em_sb[:, m : m + 1])
             nc.vector.tensor_tensor(pages[m][:].indirect(idx3[:, j0 // 16 : (j0 + n) // 16]), score[:], wgo_sb[:, j0 : j0 + n], ALU.mult)
 
         for tok in ORDER.split():
             kind = tok[0]
-            if kind == "W":
+            if kind == "B":
+                scale_bent(int(tok[2]), int(tok[3]), tok[1] == "s")
+            elif kind == "W":
                 bend(int(tok[1]), 0, S)
             elif kind == "A":
                 bend(int(tok[1]), *SLICES[int(tok[2])])

@@ -14,31 +14,24 @@ FP4X4 = mybir.dt.float4_e2m1fn_x4
 ACT = mybir.ActivationFunctionType
 ALU = mybir.AluOpType
 
+K, H, T, S, T3, S2, T2 = 1024, 1024, 2048, 512, 1024, 512, 1024
 P = 128
 PACK = 4
-K_PASS = 512
-PASSES = 2
-K, H, T, S, T3, S2, T2 = 1024, 1024, 2048, 512, 1024, 512, 1024
+K_PASS = P * PACK
+PASSES = K // K_PASS
+QUAD = 32
+QUADS = P // QUAD
 BANK = 512
-QUADS = 4
-SLICES = ((0, 256), (256, 256))
-WARM = True
-LOADS = "gain:s idx:s b1:g em:g tab0:s ts:s w1:s w1sa:s w1sb:s tab1:s idx2:s t2s:s c0:s c1:s c2:s c3:s tab2:s idx3:s wgo:s pages:s"
-FIRST = 512
-WAVE_TAG = ("wide2", "wide3")
-WAVE_AGAIN = False
-HB_TAG = ("half3", "half2", "half0", "score10")
-PACKED = False
-SHIFT_Q = "a"
-BG_TAG = ("wide0", "wide1", "half0", "half1")
-SC_TAG = {(3, 0): "wave1", (1, 0): "wave0"}
-STAGE = 3
-WAVES = 3
-ORDER = "Q0 Q1 Q2 Q3 W0 W1 Bv09 Bv19 F00 F10 G04 F01 S00 S10 F11 S20 S30 S01 S11 S21 S31"
-NB = (3, 3, 2)
-CAST_SCALAR = (0, 0, 128, 32)
+STRIPE = 16
+HALF = S // 2
+ROW_BLOCKS = S2 // P
+CHANNEL_SETS = PASSES * PACK
 
-FLOPS = 2 * K * H * S * 2 + 2 * H * S2 * S * 2
+ROUNDED_ON_SCALAR = (0, 0, 128, 60)
+BANKS_W1, BANKS_W2, BANKS_E = 3, 3, 2
+TINY = 1e-30
+
+FLOPS = 2 * (2 * K * H * S) + 2 * (2 * H * S2 * S)
 
 
 def tile_list_ballroom_exemplar_scores_kernel(
@@ -47,286 +40,223 @@ def tile_list_ballroom_exemplar_scores_kernel(
     nc = tc.nc
     with ExitStack() as ctx:
         keep = ctx.enter_context(tc.tile_pool(name="keep", bufs=1))
-        ring = ctx.enter_context(tc.tile_pool(name="ring", bufs=2))
         psum = ctx.enter_context(tc.psum_pool(name="psum", bufs=1))
 
-        def held(name, shape, dtype):
-            return keep.tile(shape, dtype, name=name, align_bytes=64)
+        def sbuf(name, shape, dtype, buffer=None):
+            return keep.tile(shape, dtype, name=name, tag=buffer or name, align_bytes=64)
 
-        idx = held("idx", [P, S // 16], U16)
-        idx2 = held("idx2", [P, S2 // 16], U16)
-        idx3 = held("idx3", [P, S // 16], U16)
-        w1_raw = held("w1_raw", [P, PASSES, H], U16)
-        w1_codes = held("w1_codes", [P, PASSES, H], U16)
-        w1_raw_scales = held("w1_raw_scales", [P, PASSES, H], U8)
-        w1_planes = held("w1_planes", [P, PASSES, H], U8)
-        tab = [held(f"tab{a}", [P, T], I32) for a in range(PASSES)]
-        tab_planes = held("tab_planes", [P, T] if PACKED else [P, PASSES, T], U8)
-        tab2 = held("tab2", [P, PASSES, T3], I32)
-        tab2_planes = held("tab2_planes", [P, T3], U8)
-        v_codes = [held(f"v_codes{a}", [P, S], I32) for a in range(PASSES)]
-        v_planes = [held(f"v_planes{a}", [P, S], U8) for a in range(PASSES)]
-        v2_codes = [held(f"v2_codes{a}", [P, S2], I32) for a in range(PASSES)]
-        v2_planes = held("v2_planes", [P, S2], U8)
+        idx = sbuf("idx", [P, S // STRIPE], U16)
+        idx2 = sbuf("idx2", [P, S2 // STRIPE], U16)
+        idx3 = sbuf("idx3", [P, S // STRIPE], U16)
+        w1_raw = sbuf("w1_raw", [P, PASSES, H], U16)
+        w1_codes = sbuf("w1_codes", [P, PASSES, H], U16)
+        w1_raw_planes = sbuf("w1_raw_planes", [P, PASSES, H], U8)
+        w1_planes = sbuf("w1_planes", [P, PASSES, H], U8)
+        tab = [sbuf(f"tab{a}", [P, T], I32) for a in range(PASSES)]
+        tab_planes = sbuf("tab_planes", [P, PASSES, T], U8)
+        tab2 = sbuf("tab2", [P, PASSES, T3], I32)
+        tab2_planes = sbuf("tab2_planes", [P, T3], U8)
+        v_codes = [sbuf(f"v_codes{a}", [P, S], I32) for a in range(PASSES)]
+        v_planes = [sbuf(f"v_planes{a}", [P, S], U8) for a in range(PASSES)]
+        v2_codes = [sbuf(f"v2_codes{a}", [P, S2], I32) for a in range(PASSES)]
+        v2_planes = sbuf("v2_planes", [P, S2], U8)
         chunks = [(b, a) for b in range(PASSES) for a in range(PASSES)]
-        w2_raw = {c: keep.tile([P, PACK, K_PASS], F32, name=f"w2_raw{c[0]}{c[1]}", tag=f"wide{i}", align_bytes=64) for i, c in enumerate(chunks)}
-        w2_bf = {c: keep.tile([P, K_PASS * PACK], BF16, name=f"w2_bf{c[0]}{c[1]}", tag=f"half{i}", align_bytes=64) for i, c in enumerate(chunks)}
-        w2_codes = {c: held(f"w2_codes{c[0]}{c[1]}", [P, K_PASS], U32) for c in chunks}
-        w2_planes = {c: held(f"w2_planes{c[0]}{c[1]}", [P, K_PASS], U8) for c in chunks}
-        pages = [held(f"page{m}", [P, T2], F32) for m in range(S2 // P)]
-        wgo_sb = held("wgo_sb", [P, S], F32)
-        gain_sb = held("gain_sb", [P, PASSES, PACK], F32)
-        b1_sb = held("b1_sb", [P, PASSES, PACK], F32)
-        em_sb = held("em_sb", [P, S2 // P], F32)
-        ones = held("ones", [P, 8], F32)
-        tiny = held("tiny", [P, 8], F32)
-        guess = held("guess", [P, 8], F32)
-        rough = held("rough", [P, 8], F32)
-        step = held("step", [P, 8], F32)
-        quarter_pi = held("quarter_pi", [P, 8], F32)
-        half_sign = held("half_sign", [P, 8], F32)
-        half_abs = held("half_abs", [P, 8], F32)
-        twice_abs = held("twice_abs", [P, 8], F32)
-        minus_abs = held("minus_abs", [P, 8], F32)
-        root = held("root", [P, 8], F32)
-        bent = [held(f"bent{b}", [P, PACK, S], F32) for b in range(PASSES)]
+        w2_raw = {c: sbuf(f"w2_raw{c[0]}{c[1]}", [P, PACK, K_PASS], F32) for c in chunks}
+        w2_bf = {c: sbuf(f"w2_bf{c[0]}{c[1]}", [P, K_PASS * PACK], BF16) for c in chunks}
+        w2_codes = {c: sbuf(f"w2_codes{c[0]}{c[1]}", [P, K_PASS], U32) for c in chunks}
+        w2_planes = {c: sbuf(f"w2_planes{c[0]}{c[1]}", [P, K_PASS], U8) for c in chunks}
+        pages = [sbuf(f"page{m}", [P, T2], F32) for m in range(ROW_BLOCKS)]
+        wgo_sb = sbuf("wgo_sb", [P, S], F32)
+        gain_sb = sbuf("gain_sb", [P, PASSES, PACK], F32)
+        b1_sb = sbuf("b1_sb", [P, PASSES, PACK], F32)
+        em_sb = sbuf("em_sb", [P, ROW_BLOCKS], F32)
+        one = sbuf("one", [P, 1], F32)
+        tiny = sbuf("tiny", [P, 1], F32)
+        quarter_pi = sbuf("quarter_pi", [P, 1], F32)
+        half_sign = sbuf("half_sign", [P, CHANNEL_SETS], F32)
+        half_abs = sbuf("half_abs", [P, CHANNEL_SETS], F32)
+        twice_abs = sbuf("twice_abs", [P, CHANNEL_SETS], F32)
+        minus_abs = sbuf("minus_abs", [P, CHANNEL_SETS], F32)
+        inverse_root = sbuf("inverse_root", [P, CHANNEL_SETS], F32)
+        rough_root = sbuf("rough_root", [P, CHANNEL_SETS], F32)
+        newton = sbuf("newton", [P, CHANNEL_SETS], F32)
+        root = sbuf("root", [P, CHANNEL_SETS], F32)
+        bent = [sbuf(f"bent{b}", [P, PACK, S], F32) for b in range(PASSES)]
 
-        nc.vector.memset((tab_planes[:] if PACKED else tab_planes[:].rearrange("p a t -> p (a t)")).bitcast(I32), 0)
-        nc.vector.memset(w1_raw_scales[:].rearrange("p a t -> p (a t)").bitcast(I32), 0)
+        nc.vector.memset(tab_planes[:].rearrange("p a t -> p (a t)").bitcast(I32), 0)
+        nc.vector.memset(w1_raw_planes[:].rearrange("p a t -> p (a t)").bitcast(I32), 0)
         nc.vector.memset(tab2_planes[:].bitcast(I32), 0)
-        nc.vector.memset(ones[:], 1.0)
-        nc.vector.tensor_scalar(tiny[:], ones[:], 1e-30, None, ALU.mult)
-        nc.vector.tensor_scalar(quarter_pi[:], ones[:], math.pi / 4, None, ALU.mult)
+        nc.vector.memset(one[:], 1.0)
+        nc.vector.tensor_scalar(tiny[:], one[:], TINY, None, ALU.mult)
+        nc.vector.tensor_scalar(quarter_pi[:], one[:], math.pi / 4, None, ALU.mult)
 
-        def load_w2(c):
-            b, a = c
+        def load_planes_side_by_side(planes, scales):
+            for s in range(PACK):
+                nc.sync.dma_start(
+                    out=planes[s:P:QUAD, :, :].bitcast(I32),
+                    in_=scales.rearrange("a (q s) t -> s q a t", s=PACK)[s].bitcast(I32),
+                )
+
+        nc.sync.dma_start(out=gain_sb[:], in_=gain.rearrange("(b p t) -> p b t", p=P, t=PACK))
+        nc.sync.dma_start(idx[:], offs)
+        nc.gpsimd.dma_start(out=b1_sb[:], in_=b1.rearrange("(b p t) -> p b t", p=P, t=PACK))
+        nc.sync.dma_start(out=tab[0][:], in_=tab_words[0].rearrange("p t i -> p (t i)").bitcast(I32))
+        load_planes_side_by_side(tab_planes, tab_scales)
+        nc.sync.dma_start(out=w1_raw[:].bitcast(I32), in_=w1_words.rearrange("a p c -> p a c").bitcast(I32))
+        load_planes_side_by_side(w1_raw_planes, w1_scales)
+        nc.sync.dma_start(out=tab[1][:], in_=tab_words[1].rearrange("p t i -> p (t i)").bitcast(I32))
+        nc.sync.dma_start(idx2[:], offs2)
+        for q in range(QUADS):
             nc.sync.dma_start(
-                out=w2_raw[c][:],
-                in_=w2[a * K_PASS : (a + 1) * K_PASS, b * K_PASS : (b + 1) * K_PASS].rearrange("(p k) r -> p k r", k=PACK),
+                out=tab2_planes[QUAD * q : QUAD * q + PASSES * PACK, :].bitcast(I32),
+                in_=tab2_scales[:, PACK * q : PACK * (q + 1), :].bitcast(I32),
             )
-
-        queues = {"s": nc.sync, "a": nc.scalar, "g": nc.gpsimd}
-
-        def load(name, q):
-            eng = queues[q]
-            if name == "idx":
-                nc.sync.dma_start(idx[:], offs)
-            elif name == "idx2":
-                nc.sync.dma_start(idx2[:], offs2)
-            elif name == "idx3":
-                nc.sync.dma_start(idx3[:], offs3)
-            elif name == "w1":
-                eng.dma_start(out=w1_raw[:].bitcast(I32), in_=w1_words.rearrange("a p c -> p a c").bitcast(I32))
-            elif name in ("tab0", "tab1"):
-                a = int(name[3:])
-                eng.dma_start(out=tab[a][:], in_=tab_words[a].rearrange("p t i -> p (t i)").bitcast(I32))
-            elif name == "ts" and PACKED:
-                for k in range(QUADS):
-                    eng.dma_start(out=tab_planes[32 * k : 32 * k + 8, :].bitcast(I32), in_=tab_scales[:, 4 * k : 4 * k + 4, :].bitcast(I32))
-            elif name == "ts":
-                for k in range(QUADS):
-                    eng.dma_start(
-                        out=tab_planes[32 * k : 32 * k + 4, :, :].bitcast(I32),
-                        in_=tab_scales[:, 4 * k : 4 * k + 4, :].rearrange("a r t -> r a t").bitcast(I32),
-                    )
-            elif name in ("w1sa", "w1sb"):
-                for k in ((0, 1) if name == "w1sa" else (2, 3)):
-                    eng.dma_start(
-                        out=w1_raw_scales[32 * k : 32 * k + 4, :, :].bitcast(I32),
-                        in_=w1_scales[:, 4 * k : 4 * k + 4, :].rearrange("a r t -> r a t").bitcast(I32),
-                    )
-            elif name == "t2s":
-                for k in range(QUADS):
-                    eng.dma_start(
-                        out=tab2_planes[32 * k : 32 * k + 8, :].bitcast(I32),
-                        in_=tab2_scales[:, 4 * k : 4 * k + 4, :].bitcast(I32),
-                    )
-            elif name == "gain":
-                eng.dma_start(out=gain_sb[:], in_=gain.rearrange("(b p t) -> p b t", p=P, t=PACK))
-            elif name == "b1":
-                eng.dma_start(out=b1_sb[:], in_=b1.rearrange("(b p t) -> p b t", p=P, t=PACK))
-            elif name == "em":
-                with nc.allow_non_contiguous_dma(reason="one factor for each partition"):
-                    eng.dma_start(out=em_sb[:], in_=em.rearrange("(m p) -> p m", p=P))
-            elif name in ("c0", "c1", "c2", "c3"):
-                load_w2(chunks[int(name[1:])])
-            elif name == "tab2":
-                eng.dma_start(out=tab2[:], in_=tab2_words.rearrange("a p t i -> p a (t i)").bitcast(I32))
-            elif name == "wgo":
-                eng.dma_start(out=wgo_sb[:], in_=wgo)
-            else:
-                for m in range(S2 // P):
-                    eng.dma_start(out=pages[m][:], in_=page1[m * P : (m + 1) * P, :])
-
-        for item in LOADS.split():
-            load(*item.split(":"))
+        for b, a in chunks:
+            rows_and_columns = w2[a * K_PASS : (a + 1) * K_PASS, b * K_PASS : (b + 1) * K_PASS]
+            nc.sync.dma_start(out=w2_raw[(b, a)][:], in_=rows_and_columns.rearrange("(p i) r -> p i r", i=PACK))
+        nc.sync.dma_start(out=tab2[:], in_=tab2_words.rearrange("a p t i -> p a (t i)").bitcast(I32))
+        with nc.allow_non_contiguous_dma(reason="one factor for each partition and row block"):
+            nc.sync.dma_start(out=em_sb[:], in_=em.rearrange("(m p) -> p m", p=P))
+        nc.sync.dma_start(idx3[:], offs3)
+        nc.sync.dma_start(out=wgo_sb[:], in_=wgo)
+        for m in range(ROW_BLOCKS):
+            nc.sync.dma_start(out=pages[m][:], in_=page1[m * P : (m + 1) * P, :])
 
         gain_flat = gain_sb[:].rearrange("p b t -> p (b t)")
         nc.gpsimd.tensor_scalar(half_sign[:], gain_flat, 0.0, -0.5, ALU.is_ge, ALU.add)
         nc.gpsimd.tensor_tensor(half_abs[:], gain_flat, half_sign[:], ALU.mult)
         nc.gpsimd.tensor_scalar(twice_abs[:], half_abs[:], 4.0, 0.0, ALU.mult, ALU.add)
         nc.gpsimd.tensor_scalar(minus_abs[:], half_abs[:], -2.0, 0.0, ALU.mult, ALU.add)
-        nc.scalar.activation(out=guess[:], in_=gain_flat, func=ACT.Abs_reciprocal_sqrt, scale=2.0, bias=tiny[:, 0:1])
-        if WARM:
-            warm = held("warm", [P, 1], F32)
-            nc.scalar.activation(out=warm[:], in_=guess[:, 0:1], func=ACT.Silu)
-        nc.gpsimd.tensor_tensor(rough[:], twice_abs[:], guess[:], ALU.mult)
-        nc.gpsimd.tensor_tensor(step[:], rough[:], guess[:], ALU.mult)
-        nc.gpsimd.tensor_scalar(step[:], step[:], -0.5, 1.5, ALU.mult, ALU.add)
-        nc.gpsimd.tensor_tensor(root[:], rough[:], step[:], ALU.mult)
+        nc.scalar.activation(out=inverse_root[:], in_=gain_flat, func=ACT.Abs_reciprocal_sqrt, scale=2.0, bias=tiny[:])
+        warm = sbuf("warm", [P, 1], F32)
+        nc.scalar.activation(out=warm[:], in_=inverse_root[:, 0:1], func=ACT.Silu)
+        nc.gpsimd.tensor_tensor(rough_root[:], twice_abs[:], inverse_root[:], ALU.mult)
+        nc.gpsimd.tensor_tensor(newton[:], rough_root[:], inverse_root[:], ALU.mult)
+        nc.gpsimd.tensor_scalar(newton[:], newton[:], -0.5, 1.5, ALU.mult, ALU.add)
+        nc.gpsimd.tensor_tensor(root[:], rough_root[:], newton[:], ALU.mult)
 
         nc.scalar.copy(
             out=w1_codes[:].rearrange("p a (b t m) -> p (a b) t m", t=PACK, m=P),
             in_=w1_raw[:].rearrange("p a (b m t) -> p (a b) t m", t=PACK, m=P),
         )
-        def gather_v(j0, j1):
-            part = idx[:, j0 // 16 : j1 // 16]
-            nc.vector.tensor_copy(v_codes[0][:, j0:j1].bitcast(U32), tab[0][:].bitcast(U32).indirect(part))
-            if PACKED:
-                nc.vector.tensor_copy(v_planes[0][:, j0:j1], tab_planes[:].indirect(part))
-                queues[SHIFT_Q].dma_start(out=v_planes[1][0 : P - 4, j0:j1].bitcast(I32), in_=v_planes[0][4:P, j0:j1].bitcast(I32))
-            else:
-                for a in range(PASSES):
-                    nc.vector.tensor_copy(v_planes[a][:, j0:j1], tab_planes[:, a, :].indirect(part))
-            if j0 == 0:
-                nc.vector.tensor_copy(
-                    out=w1_planes[:].rearrange("p a (b t m) -> p (a b) t m", t=PACK, m=P),
-                    in_=w1_raw_scales[:].rearrange("p a (b m t) -> p (a b) t m", t=PACK, m=P),
-                )
-            nc.vector.tensor_copy(v_codes[1][:, j0:j1].bitcast(U32), tab[1][:].bitcast(U32).indirect(part))
-
-        gather_v(0, FIRST)
-        if FIRST < S:
-            gather_v(FIRST, S)
+        nc.vector.tensor_copy(v_codes[0][:].bitcast(U32), tab[0][:].bitcast(U32).indirect(idx[:]))
+        for a in range(PASSES):
+            nc.vector.tensor_copy(v_planes[a][:], tab_planes[:, a, :].indirect(idx[:]))
+        nc.vector.tensor_copy(
+            out=w1_planes[:].rearrange("p a (b t m) -> p (a b) t m", t=PACK, m=P),
+            in_=w1_raw_planes[:].rearrange("p a (b m t) -> p (a b) t m", t=PACK, m=P),
+        )
+        nc.vector.tensor_copy(v_codes[1][:].bitcast(U32), tab[1][:].bitcast(U32).indirect(idx[:]))
         nc.vector.tensor_copy(v2_planes[:], tab2_planes[:].indirect(idx2[:]))
 
-        def quantize_w2(c):
-            n_s = CAST_SCALAR[chunks.index(c)]
-            src = w2_raw[c][:].rearrange("p k (m u t) -> p u m k t", u=2, t=2)
-            dst = w2_bf[c][:].rearrange("p (u t m k) -> p u m k t", u=2, t=2, k=PACK)
-            if n_s > 0:
-                nc.scalar.copy(out=dst[:, :, 0:n_s], in_=src[:, :, 0:n_s])
-            if n_s < P:
-                nc.vector.tensor_copy(out=dst[:, :, n_s:P], in_=src[:, :, n_s:P])
+        def quantize_w2(c, on_scalar):
+            src = w2_raw[c][:].rearrange("p i (m u t) -> p u m i t", u=2, t=2)
+            dst = w2_bf[c][:].rearrange("p (u t m i) -> p u m i t", u=2, t=2, i=PACK)
+            if on_scalar > 0:
+                nc.scalar.copy(out=dst[:, :, 0:on_scalar], in_=src[:, :, 0:on_scalar])
+            if on_scalar < P:
+                nc.vector.tensor_copy(out=dst[:, :, on_scalar:P], in_=src[:, :, on_scalar:P])
             nc.vector.quantize_mx(out=w2_codes[c][:].bitcast(FP8X4), scales=w2_planes[c][:], in_=w2_bf[c][:])
 
-        scaled = {}
+        def bend(b):
+            for t in range(PACK):
+                acc = psum.tile([P, S], F32, name="acc_w1", tag="acc_w1", bufs=BANKS_W1)
+                places = slice(b * K_PASS + t * P, b * K_PASS + (t + 1) * P)
+                for a in range(PASSES):
+                    nc.tensor.matmul_mx(
+                        out=acc[:],
+                        lhsT=w1_codes[:, a, places].bitcast(FP4X4),
+                        lhsT_scale=w1_planes[:, a, places],
+                        rhs=v_codes[a][:].bitcast(FP8X4),
+                        rhs_scale=v_planes[a][:],
+                        start=(a == 0),
+                        stop=(a == PASSES - 1),
+                    )
+                nc.scalar.activation(out=bent[b][:, t, :], in_=acc[:], func=ACT.Tanh, bias=b1_sb[:, b, t : t + 1])
 
-        def bend(b, j0, n):
-            per_bank = BANK // n
-            for t0 in range(0, PACK, per_bank):
-                acc = psum.tile([P, per_bank, n], F32, name="acc1", tag="acc1", bufs=NB[0])
-                for u in range(per_bank):
-                    cols = slice(b * K_PASS + (t0 + u) * P, b * K_PASS + (t0 + u + 1) * P)
-                    for a in range(PASSES):
-                        nc.tensor.matmul_mx(
-                            out=acc[:, u, :],
-                            lhsT=w1_codes[:, a, cols].bitcast(FP4X4),
-                            lhsT_scale=w1_planes[:, a, cols],
-                            rhs=v_codes[a][:, j0 : j0 + n].bitcast(FP8X4),
-                            rhs_scale=v_planes[a][:, j0 : j0 + n],
-                            start=(a == 0),
-                            stop=(a == PASSES - 1),
-                        )
-                for u in range(per_bank):
-                    t = t0 + u
-                    nc.scalar.activation(out=bent[b][:, t, j0 : j0 + n], in_=acc[:, u, :], func=ACT.Tanh, bias=b1_sb[:, b, t : t + 1])
-
-        def scale_bent(b, i, on_scalar):
-            j0, n = SLICES[i] if i < 9 else (0, S)
-            whole = keep.tile([P, PACK, n], F32, name=f"scaled{b}{i}", tag=BG_TAG[2 * (i % 9) + b], align_bytes=64)
-            for j, w in SLICES:
-                if j0 <= j < j0 + n:
-                    scaled[(b, j)] = whole[:, :, j - j0 : j - j0 + w]
+        def scale_bent(b):
+            scaled = sbuf(f"scaled{b}", [P, PACK, S], F32, buffer=f"w2_raw0{b}")
             for t in range(PACK):
                 ch = b * PACK + t
-                part = bent[b][:, t, j0 : j0 + n]
-                dest = whole[:, t, :]
-                if on_scalar:
-                    nc.scalar.activation(out=dest, in_=part, func=ACT.Identity, scale=gain_sb[:, b, t : t + 1], bias=minus_abs[:, ch : ch + 1])
-                else:
-                    nc.vector.tensor_scalar(dest, part, gain_sb[:, b, t : t + 1], minus_abs[:, ch : ch + 1], ALU.mult, ALU.add)
+                nc.vector.tensor_scalar(
+                    scaled[:, t, :], bent[b][:, t, :], gain_sb[:, b, t : t + 1], minus_abs[:, ch : ch + 1], ALU.mult, ALU.add
+                )
+            return scaled
 
-        h_codes = {}
-        h_planes = {}
-
-        def features(b, j0, n):
-            per_bank = BANK // n
-            wave = keep.tile([P, PACK, n], F32, name="wave", tag=WAVE_TAG[b] if j0 == 0 or WAVE_AGAIN else f"wave{b}", align_bytes=64)
+        def features(b, half, scaled, wave_buffer, h_buffer):
+            dances = slice(half * HALF, (half + 1) * HALF)
+            per_bank = BANK // HALF
+            wave = sbuf("wave", [P, PACK, HALF], F32, buffer=wave_buffer)
             for t0 in range(0, PACK, per_bank):
-                acc = psum.tile([P, per_bank, n], F32, name="acc2", tag="acc2", bufs=NB[1])
+                acc = psum.tile([P, per_bank, HALF], F32, name="acc_w2", tag="acc_w2", bufs=BANKS_W2)
                 for u in range(per_bank):
-                    cols = slice((t0 + u) * P, (t0 + u + 1) * P)
+                    places = slice((t0 + u) * P, (t0 + u + 1) * P)
                     for a in range(PASSES):
                         nc.tensor.matmul_mx(
                             out=acc[:, u, :],
-                            lhsT=w2_codes[(b, a)][:, cols].bitcast(FP8X4),
-                            lhsT_scale=w2_planes[(b, a)][:, cols],
-                            rhs=v_codes[a][:, j0 : j0 + n].bitcast(FP8X4),
-                            rhs_scale=v_planes[a][:, j0 : j0 + n],
+                            lhsT=w2_codes[(b, a)][:, places].bitcast(FP8X4),
+                            lhsT_scale=w2_planes[(b, a)][:, places],
+                            rhs=v_codes[a][:, dances].bitcast(FP8X4),
+                            rhs_scale=v_planes[a][:, dances],
                             start=(a == 0),
                             stop=(a == PASSES - 1),
                         )
                 for u in range(per_bank):
-                    t = t0 + u
-                    ch = b * PACK + t
+                    ch = b * PACK + t0 + u
                     nc.scalar.activation(
-                        out=wave[:, t, :], in_=acc[:, u, :], func=ACT.Sin, scale=half_sign[:, ch : ch + 1], bias=quarter_pi[:, 0:1]
+                        out=wave[:, t0 + u, :], in_=acc[:, u, :], func=ACT.Sin, scale=half_sign[:, ch : ch + 1], bias=quarter_pi[:]
                     )
                 for u in range(per_bank):
-                    t = t0 + u
-                    ch = b * PACK + t
-                    nc.scalar.activation(out=wave[:, t, :], in_=wave[:, t, :], func=ACT.Square, scale=root[:, ch : ch + 1])
-            h_bf = keep.tile([P, n * PACK], BF16, name="h_bf", tag=HB_TAG[2 * [j for j, w in SLICES].index(j0) + b], align_bytes=64)
+                    ch = b * PACK + t0 + u
+                    nc.scalar.activation(out=wave[:, t0 + u, :], in_=wave[:, t0 + u, :], func=ACT.Square, scale=root[:, ch : ch + 1])
+            h_bf = sbuf("h_bf", [P, HALF * PACK], BF16, buffer=h_buffer)
             nc.vector.tensor_tensor(
-                h_bf[:].rearrange("p (c i t) -> p c t i", i=2, t=PACK),
-                wave[:].rearrange("p t (c i) -> p c t i", i=2),
-                scaled[(b, j0)].rearrange("p t (c i) -> p c t i", i=2),
+                h_bf[:].rearrange("p (c e t) -> p c t e", e=2, t=PACK),
+                wave[:].rearrange("p t (c e) -> p c t e", e=2),
+                scaled[:, :, dances].rearrange("p t (c e) -> p c t e", e=2),
                 ALU.add,
             )
-            h_codes[(b, j0)] = held(f"h_codes{b}_{j0}", [P, n], U32)
-            h_planes[(b, j0)] = held(f"h_planes{b}_{j0}", [P, n], U8)
-            nc.vector.quantize_mx(out=h_codes[(b, j0)][:].bitcast(FP8X4), scales=h_planes[(b, j0)][:], in_=h_bf[:])
+            h_codes = sbuf(f"h_codes{b}{half}", [P, HALF], U32)
+            h_plane = sbuf(f"h_plane{b}{half}", [P, HALF], U8)
+            nc.vector.quantize_mx(out=h_codes[:].bitcast(FP8X4), scales=h_plane[:], in_=h_bf[:])
+            return h_codes[:], h_plane[:]
 
-        def scores(m, j0, n):
-            rows = slice(m * P, (m + 1) * P)
-            acc = psum.tile([P, n], F32, name="acc3", tag="acc3", bufs=NB[2])
-            moving = [(a, v_codes[a][:, j0 : j0 + n], v_planes[a][:, j0 : j0 + n]) for a in range(PASSES)]
-            moving = moving + [(a, h_codes[(a, j0)][:], h_planes[(a, j0)][:]) for a in range(PASSES)]
-            for i, (a, codes, planes) in enumerate(moving):
+        def scores(m, half, h, score_buffer):
+            dances = slice(half * HALF, (half + 1) * HALF)
+            exemplars = slice(m * P, (m + 1) * P)
+            acc = psum.tile([P, HALF], F32, name="acc_e", tag="acc_e", bufs=BANKS_E)
+            moving = [(a, v_codes[a][:, dances], v_planes[a][:, dances]) for a in range(PASSES)]
+            moving = moving + [(b, *h[b]) for b in range(PASSES)]
+            for n, (a, codes, plane) in enumerate(moving):
                 nc.tensor.matmul_mx(
                     out=acc[:],
-                    lhsT=v2_codes[a][:, rows].bitcast(FP8X4),
-                    lhsT_scale=v2_planes[4 * a : P, rows],
+                    lhsT=v2_codes[a][:, exemplars].bitcast(FP8X4),
+                    lhsT_scale=v2_planes[PACK * a : P, exemplars],
                     rhs=codes.bitcast(FP8X4),
-                    rhs_scale=planes,
-                    start=(i == 0),
-                    stop=(i == len(moving) - 1),
+                    rhs_scale=plane,
+                    start=(n == 0),
+                    stop=(n == len(moving) - 1),
                 )
-            score = keep.tile([P, n], F32, name="score", tag=SC_TAG.get((m, j0), f"score{m}{[j for j, w in SLICES].index(j0)}"), align_bytes=64)
+            score = sbuf("score", [P, HALF], F32, buffer=score_buffer)
             nc.scalar.activation(out=score[:], in_=acc[:], func=ACT.Tanh, scale=em_sb[:, m : m + 1])
-            nc.vector.tensor_tensor(pages[m][:].indirect(idx3[:, j0 // 16 : (j0 + n) // 16]), score[:], wgo_sb[:, j0 : j0 + n], ALU.mult)
+            entries = idx3[:, half * HALF // STRIPE : (half + 1) * HALF // STRIPE]
+            nc.vector.tensor_tensor(pages[m][:].indirect(entries), score[:], wgo_sb[:, dances], ALU.mult)
 
-        for tok in ORDER.split():
-            kind = tok[0]
-            if kind == "B":
-                scale_bent(int(tok[2]), int(tok[3]), tok[1] == "s")
-            elif kind == "W":
-                bend(int(tok[1]), 0, S)
-            elif kind == "A":
-                bend(int(tok[1]), *SLICES[int(tok[2])])
-            elif kind == "Q":
-                quantize_w2(chunks[int(tok[1])])
-            elif kind == "F":
-                features(int(tok[1]), *SLICES[int(tok[2])])
-            elif kind == "G":
-                for a in range(PASSES):
-                    m0, m1 = int(tok[1]), int(tok[2])
-                    nc.vector.tensor_copy(
-                        v2_codes[a][:, m0 * P : m1 * P].bitcast(U32), tab2[:, a, :].bitcast(U32).indirect(idx2[:, m0 * 8 : m1 * 8])
-                    )
-            else:
-                m = int(tok[1])
-                scores(m, *SLICES[int(tok[2])])
-                if int(tok[2]) == len(SLICES) - 1:
-                    nc.sync.dma_start(out=out[m * P : (m + 1) * P, :], in_=pages[m][:])
+        for c, on_scalar in zip(chunks, ROUNDED_ON_SCALAR):
+            quantize_w2(c, on_scalar)
+        for b in range(PASSES):
+            bend(b)
+        scaled = [scale_bent(b) for b in range(PASSES)]
+
+        first = [features(b, 0, scaled[b], f"w2_raw1{b}", f"w2_bf1{1 - b}") for b in range(PASSES)]
+        for a in range(PASSES):
+            nc.vector.tensor_copy(v2_codes[a][:].bitcast(U32), tab2[:, a, :].bitcast(U32).indirect(idx2[:]))
+
+        second = []
+        for b in range(PASSES):
+            second.append(features(b, 1, scaled[b], f"late_wave{b}", "w2_bf00" if b == 0 else "late_h"))
+            scores(2 * b, 0, first, f"score{2 * b}")
+            scores(2 * b + 1, 0, first, f"late_wave{b}")
+        for m in range(ROW_BLOCKS):
+            scores(m, 1, second, f"late_score{m}")
+            nc.sync.dma_start(out=out[m * P : (m + 1) * P, :], in_=pages[m][:])

import math
from contextlib import ExitStack

import concourse.mybir as mybir

F32 = mybir.dt.float32
BF16 = mybir.dt.bfloat16
I32 = mybir.dt.int32
U32 = mybir.dt.uint32
U16 = mybir.dt.uint16
U8 = mybir.dt.uint8
FP8X4 = mybir.dt.float8_e4m3fn_x4
FP4X4 = mybir.dt.float4_e2m1fn_x4
ACT = mybir.ActivationFunctionType
ALU = mybir.AluOpType

K, H, T, S, T3, S2, T2 = 1024, 1024, 2048, 512, 1024, 512, 1024
P = 128
PACK = 4
K_PASS = P * PACK
PASSES = K // K_PASS
QUAD = 32
QUADS = P // QUAD
BANK = 512
STRIPE = 16
HALF = S // 2
ROW_BLOCKS = S2 // P
CHANNEL_SETS = PASSES * PACK

ROUNDED_ON_SCALAR = (0, 0, 128, 60)
BANKS_W1, BANKS_W2, BANKS_E = 3, 3, 2
TINY = 1e-30

FLOPS = 2 * (2 * K * H * S) + 2 * (2 * H * S2 * S)


def tile_list_ballroom_exemplar_scores_kernel(
    tc, tab_words, tab_scales, offs, tab2_words, tab2_scales, offs2, offs3, w1_words, w1_scales, b1, w2, gain, em, page1, wgo, out
):
    nc = tc.nc
    with ExitStack() as ctx:
        keep = ctx.enter_context(tc.tile_pool(name="keep", bufs=1))
        psum = ctx.enter_context(tc.psum_pool(name="psum", bufs=1))

        def sbuf(name, shape, dtype, buffer=None):
            return keep.tile(shape, dtype, name=name, tag=buffer or name, align_bytes=64)

        idx = sbuf("idx", [P, S // STRIPE], U16)
        idx2 = sbuf("idx2", [P, S2 // STRIPE], U16)
        idx3 = sbuf("idx3", [P, S // STRIPE], U16)
        w1_raw = sbuf("w1_raw", [P, PASSES, H], U16)
        w1_codes = sbuf("w1_codes", [P, PASSES, H], U16)
        w1_raw_planes = sbuf("w1_raw_planes", [P, PASSES, H], U8)
        w1_planes = sbuf("w1_planes", [P, PASSES, H], U8)
        tab = [sbuf(f"tab{a}", [P, T], I32) for a in range(PASSES)]
        tab_planes = sbuf("tab_planes", [P, PASSES, T], U8)
        tab2 = sbuf("tab2", [P, PASSES, T3], I32)
        tab2_planes = sbuf("tab2_planes", [P, T3], U8)
        v_codes = [sbuf(f"v_codes{a}", [P, S], I32) for a in range(PASSES)]
        v_planes = [sbuf(f"v_planes{a}", [P, S], U8) for a in range(PASSES)]
        v2_codes = [sbuf(f"v2_codes{a}", [P, S2], I32) for a in range(PASSES)]
        v2_planes = sbuf("v2_planes", [P, S2], U8)
        chunks = [(b, a) for b in range(PASSES) for a in range(PASSES)]
        w2_raw = {c: sbuf(f"w2_raw{c[0]}{c[1]}", [P, PACK, K_PASS], F32) for c in chunks}
        w2_bf = {c: sbuf(f"w2_bf{c[0]}{c[1]}", [P, K_PASS * PACK], BF16) for c in chunks}
        w2_codes = {c: sbuf(f"w2_codes{c[0]}{c[1]}", [P, K_PASS], U32) for c in chunks}
        w2_planes = {c: sbuf(f"w2_planes{c[0]}{c[1]}", [P, K_PASS], U8) for c in chunks}
        pages = [sbuf(f"page{m}", [P, T2], F32) for m in range(ROW_BLOCKS)]
        wgo_sb = sbuf("wgo_sb", [P, S], F32)
        gain_sb = sbuf("gain_sb", [P, PASSES, PACK], F32)
        b1_sb = sbuf("b1_sb", [P, PASSES, PACK], F32)
        em_sb = sbuf("em_sb", [P, ROW_BLOCKS], F32)
        one = sbuf("one", [P, 1], F32)
        tiny = sbuf("tiny", [P, 1], F32)
        quarter_pi = sbuf("quarter_pi", [P, 1], F32)
        half_sign = sbuf("half_sign", [P, CHANNEL_SETS], F32)
        half_abs = sbuf("half_abs", [P, CHANNEL_SETS], F32)
        twice_abs = sbuf("twice_abs", [P, CHANNEL_SETS], F32)
        minus_abs = sbuf("minus_abs", [P, CHANNEL_SETS], F32)
        inverse_root = sbuf("inverse_root", [P, CHANNEL_SETS], F32)
        rough_root = sbuf("rough_root", [P, CHANNEL_SETS], F32)
        newton = sbuf("newton", [P, CHANNEL_SETS], F32)
        root = sbuf("root", [P, CHANNEL_SETS], F32)
        bent = [sbuf(f"bent{b}", [P, PACK, S], F32) for b in range(PASSES)]

        nc.vector.memset(tab_planes[:].rearrange("p a t -> p (a t)").bitcast(I32), 0)
        nc.vector.memset(w1_raw_planes[:].rearrange("p a t -> p (a t)").bitcast(I32), 0)
        nc.vector.memset(tab2_planes[:].bitcast(I32), 0)
        nc.vector.memset(one[:], 1.0)
        nc.vector.tensor_scalar(tiny[:], one[:], TINY, None, ALU.mult)
        nc.vector.tensor_scalar(quarter_pi[:], one[:], math.pi / 4, None, ALU.mult)

        def load_planes_side_by_side(planes, scales):
            for s in range(PACK):
                nc.sync.dma_start(
                    out=planes[s:P:QUAD, :, :].bitcast(I32),
                    in_=scales.rearrange("a (q s) t -> s q a t", s=PACK)[s].bitcast(I32),
                )

        nc.sync.dma_start(out=gain_sb[:], in_=gain.rearrange("(b p t) -> p b t", p=P, t=PACK))
        nc.sync.dma_start(idx[:], offs)
        nc.gpsimd.dma_start(out=b1_sb[:], in_=b1.rearrange("(b p t) -> p b t", p=P, t=PACK))
        nc.sync.dma_start(out=tab[0][:], in_=tab_words[0].rearrange("p t i -> p (t i)").bitcast(I32))
        load_planes_side_by_side(tab_planes, tab_scales)
        nc.sync.dma_start(out=w1_raw[:].bitcast(I32), in_=w1_words.rearrange("a p c -> p a c").bitcast(I32))
        load_planes_side_by_side(w1_raw_planes, w1_scales)
        nc.sync.dma_start(out=tab[1][:], in_=tab_words[1].rearrange("p t i -> p (t i)").bitcast(I32))
        nc.sync.dma_start(idx2[:], offs2)
        for q in range(QUADS):
            nc.sync.dma_start(
                out=tab2_planes[QUAD * q : QUAD * q + PASSES * PACK, :].bitcast(I32),
                in_=tab2_scales[:, PACK * q : PACK * (q + 1), :].bitcast(I32),
            )
        for b, a in chunks:
            rows_and_columns = w2[a * K_PASS : (a + 1) * K_PASS, b * K_PASS : (b + 1) * K_PASS]
            nc.sync.dma_start(out=w2_raw[(b, a)][:], in_=rows_and_columns.rearrange("(p i) r -> p i r", i=PACK))
        nc.sync.dma_start(out=tab2[:], in_=tab2_words.rearrange("a p t i -> p a (t i)").bitcast(I32))
        with nc.allow_non_contiguous_dma(reason="one factor for each partition and row block"):
            nc.sync.dma_start(out=em_sb[:], in_=em.rearrange("(m p) -> p m", p=P))
        nc.sync.dma_start(idx3[:], offs3)
        nc.sync.dma_start(out=wgo_sb[:], in_=wgo)
        for m in range(ROW_BLOCKS):
            nc.sync.dma_start(out=pages[m][:], in_=page1[m * P : (m + 1) * P, :])

        gain_flat = gain_sb[:].rearrange("p b t -> p (b t)")
        nc.gpsimd.tensor_scalar(half_sign[:], gain_flat, 0.0, -0.5, ALU.is_ge, ALU.add)
        nc.gpsimd.tensor_tensor(half_abs[:], gain_flat, half_sign[:], ALU.mult)
        nc.gpsimd.tensor_scalar(twice_abs[:], half_abs[:], 4.0, 0.0, ALU.mult, ALU.add)
        nc.gpsimd.tensor_scalar(minus_abs[:], half_abs[:], -2.0, 0.0, ALU.mult, ALU.add)
        nc.scalar.activation(out=inverse_root[:], in_=gain_flat, func=ACT.Abs_reciprocal_sqrt, scale=2.0, bias=tiny[:])
        warm = sbuf("warm", [P, 1], F32)
        nc.scalar.activation(out=warm[:], in_=inverse_root[:, 0:1], func=ACT.Silu)
        nc.gpsimd.tensor_tensor(rough_root[:], twice_abs[:], inverse_root[:], ALU.mult)
        nc.gpsimd.tensor_tensor(newton[:], rough_root[:], inverse_root[:], ALU.mult)
        nc.gpsimd.tensor_scalar(newton[:], newton[:], -0.5, 1.5, ALU.mult, ALU.add)
        nc.gpsimd.tensor_tensor(root[:], rough_root[:], newton[:], ALU.mult)

        nc.scalar.copy(
            out=w1_codes[:].rearrange("p a (b t m) -> p (a b) t m", t=PACK, m=P),
            in_=w1_raw[:].rearrange("p a (b m t) -> p (a b) t m", t=PACK, m=P),
        )
        nc.vector.tensor_copy(v_codes[0][:].bitcast(U32), tab[0][:].bitcast(U32).indirect(idx[:]))
        for a in range(PASSES):
            nc.vector.tensor_copy(v_planes[a][:], tab_planes[:, a, :].indirect(idx[:]))
        nc.vector.tensor_copy(
            out=w1_planes[:].rearrange("p a (b t m) -> p (a b) t m", t=PACK, m=P),
            in_=w1_raw_planes[:].rearrange("p a (b m t) -> p (a b) t m", t=PACK, m=P),
        )
        nc.vector.tensor_copy(v_codes[1][:].bitcast(U32), tab[1][:].bitcast(U32).indirect(idx[:]))
        nc.vector.tensor_copy(v2_planes[:], tab2_planes[:].indirect(idx2[:]))

        def quantize_w2(c, on_scalar):
            src = w2_raw[c][:].rearrange("p i (m u t) -> p u m i t", u=2, t=2)
            dst = w2_bf[c][:].rearrange("p (u t m i) -> p u m i t", u=2, t=2, i=PACK)
            if on_scalar > 0:
                nc.scalar.copy(out=dst[:, :, 0:on_scalar], in_=src[:, :, 0:on_scalar])
            if on_scalar < P:
                nc.vector.tensor_copy(out=dst[:, :, on_scalar:P], in_=src[:, :, on_scalar:P])
            nc.vector.quantize_mx(out=w2_codes[c][:].bitcast(FP8X4), scales=w2_planes[c][:], in_=w2_bf[c][:])

        def bend(b):
            for t in range(PACK):
                acc = psum.tile([P, S], F32, name="acc_w1", tag="acc_w1", bufs=BANKS_W1)
                places = slice(b * K_PASS + t * P, b * K_PASS + (t + 1) * P)
                for a in range(PASSES):
                    nc.tensor.matmul_mx(
                        out=acc[:],
                        lhsT=w1_codes[:, a, places].bitcast(FP4X4),
                        lhsT_scale=w1_planes[:, a, places],
                        rhs=v_codes[a][:].bitcast(FP8X4),
                        rhs_scale=v_planes[a][:],
                        start=(a == 0),
                        stop=(a == PASSES - 1),
                    )
                nc.scalar.activation(out=bent[b][:, t, :], in_=acc[:], func=ACT.Tanh, bias=b1_sb[:, b, t : t + 1])

        def scale_bent(b):
            scaled = sbuf(f"scaled{b}", [P, PACK, S], F32, buffer=f"w2_raw0{b}")
            for t in range(PACK):
                ch = b * PACK + t
                nc.vector.tensor_scalar(
                    scaled[:, t, :], bent[b][:, t, :], gain_sb[:, b, t : t + 1], minus_abs[:, ch : ch + 1], ALU.mult, ALU.add
                )
            return scaled

        def features(b, half, scaled, wave_buffer, h_buffer):
            dances = slice(half * HALF, (half + 1) * HALF)
            per_bank = BANK // HALF
            wave = sbuf("wave", [P, PACK, HALF], F32, buffer=wave_buffer)
            for t0 in range(0, PACK, per_bank):
                acc = psum.tile([P, per_bank, HALF], F32, name="acc_w2", tag="acc_w2", bufs=BANKS_W2)
                for u in range(per_bank):
                    places = slice((t0 + u) * P, (t0 + u + 1) * P)
                    for a in range(PASSES):
                        nc.tensor.matmul_mx(
                            out=acc[:, u, :],
                            lhsT=w2_codes[(b, a)][:, places].bitcast(FP8X4),
                            lhsT_scale=w2_planes[(b, a)][:, places],
                            rhs=v_codes[a][:, dances].bitcast(FP8X4),
                            rhs_scale=v_planes[a][:, dances],
                            start=(a == 0),
                            stop=(a == PASSES - 1),
                        )
                for u in range(per_bank):
                    ch = b * PACK + t0 + u
                    nc.scalar.activation(
                        out=wave[:, t0 + u, :], in_=acc[:, u, :], func=ACT.Sin, scale=half_sign[:, ch : ch + 1], bias=quarter_pi[:]
                    )
                for u in range(per_bank):
                    ch = b * PACK + t0 + u
                    nc.scalar.activation(out=wave[:, t0 + u, :], in_=wave[:, t0 + u, :], func=ACT.Square, scale=root[:, ch : ch + 1])
            h_bf = sbuf("h_bf", [P, HALF * PACK], BF16, buffer=h_buffer)
            nc.vector.tensor_tensor(
                h_bf[:].rearrange("p (c e t) -> p c t e", e=2, t=PACK),
                wave[:].rearrange("p t (c e) -> p c t e", e=2),
                scaled[:, :, dances].rearrange("p t (c e) -> p c t e", e=2),
                ALU.add,
            )
            h_codes = sbuf(f"h_codes{b}{half}", [P, HALF], U32)
            h_plane = sbuf(f"h_plane{b}{half}", [P, HALF], U8)
            nc.vector.quantize_mx(out=h_codes[:].bitcast(FP8X4), scales=h_plane[:], in_=h_bf[:])
            return h_codes[:], h_plane[:]

        def scores(m, half, h, score_buffer):
            dances = slice(half * HALF, (half + 1) * HALF)
            exemplars = slice(m * P, (m + 1) * P)
            acc = psum.tile([P, HALF], F32, name="acc_e", tag="acc_e", bufs=BANKS_E)
            moving = [(a, v_codes[a][:, dances], v_planes[a][:, dances]) for a in range(PASSES)]
            moving = moving + [(b, *h[b]) for b in range(PASSES)]
            for n, (a, codes, plane) in enumerate(moving):
                nc.tensor.matmul_mx(
                    out=acc[:],
                    lhsT=v2_codes[a][:, exemplars].bitcast(FP8X4),
                    lhsT_scale=v2_planes[PACK * a : P, exemplars],
                    rhs=codes.bitcast(FP8X4),
                    rhs_scale=plane,
                    start=(n == 0),
                    stop=(n == len(moving) - 1),
                )
            score = sbuf("score", [P, HALF], F32, buffer=score_buffer)
            nc.scalar.activation(out=score[:], in_=acc[:], func=ACT.Tanh, scale=em_sb[:, m : m + 1])
            entries = idx3[:, half * HALF // STRIPE : (half + 1) * HALF // STRIPE]
            nc.vector.tensor_tensor(pages[m][:].indirect(entries), score[:], wgo_sb[:, dances], ALU.mult)

        for c, on_scalar in zip(chunks, ROUNDED_ON_SCALAR):
            quantize_w2(c, on_scalar)
        for b in range(PASSES):
            bend(b)
        scaled = [scale_bent(b) for b in range(PASSES)]

        first = [features(b, 0, scaled[b], f"w2_raw1{b}", f"w2_bf1{1 - b}") for b in range(PASSES)]
        for a in range(PASSES):
            nc.vector.tensor_copy(v2_codes[a][:].bitcast(U32), tab2[:, a, :].bitcast(U32).indirect(idx2[:]))

        second = []
        for b in range(PASSES):
            second.append(features(b, 1, scaled[b], f"late_wave{b}", "w2_bf00" if b == 0 else "late_h"))
            scores(2 * b, 0, first, f"score{2 * b}")
            scores(2 * b + 1, 0, first, f"late_wave{b}")
        for m in range(ROW_BLOCKS):
            scores(m, 1, second, f"late_score{m}")
            nc.sync.dma_start(out=out[m * P : (m + 1) * P, :], in_=pages[m][:])
